import numpy as np
import ml_dtypes


def mxq(x, axis, fmt="e4m3"):
    dtype, down = {"e4m3": (ml_dtypes.float8_e4m3fn, 7), "e5m2": (ml_dtypes.float8_e5m2, 14)}[fmt]
    v = np.moveaxis(np.asarray(x, np.float32).astype(ml_dtypes.bfloat16).astype(np.float64), axis, -1)
    blocks = v.reshape(v.shape[:-1] + (-1, 32))
    amax = np.abs(blocks).max(-1, keepdims=True)
    byte = np.maximum(np.where(amax > 0, np.frexp(amax)[1] - 1 + 127, 0) - down, 1)
    scale = np.exp2(byte - 127.0)
    codes = (blocks / scale).astype(np.float32).astype(dtype).astype(np.float64)
    return np.moveaxis((codes * scale).reshape(v.shape), -1, axis)


WIDE = False


def mx_kscale(k):
    if not WIDE:
        return np.ones(k)
    levels = np.array([30, -30])
    if k % 512:
        return np.exp2(np.random.permutation(np.resize(levels, k // 32))).repeat(32)
    a = np.empty((k // 512, 16))
    for p in range(k // 512):
        a[p, :8] = np.random.permutation(np.resize(levels, 8))
        for g in range(8):
            far = levels[np.abs(levels - a[p, g]) >= 10]
            a[p, g + 8] = far[np.random.randint(len(far))]
    return np.exp2(a.ravel()).repeat(32)


def f64(x):
    return np.asarray(x).astype(np.float64)


def striped(idx):
    return np.tile(np.asarray(idx).reshape(-1, 16).T, (8, 1)).astype(np.uint16)


def unstriped(offs):
    return offs[:16].T.reshape(-1).astype(np.int64)


E2M1 = np.array([0.0, 0.5, 1.0, 1.5, 2.0, 3.0, 4.0, 6.0, -0.0, -0.5, -1.0, -1.5, -2.0, -3.0, -4.0, -6.0])


def pack_weight(w, fmt):
    k, n = w.shape
    w = f64(np.asarray(w, np.float32).astype(ml_dtypes.bfloat16)).reshape(k // 32, 32, n)
    amax = np.abs(w).max(1)
    if fmt in ("e4m3", "e5m2"):
        byte = np.frexp(amax)[1] - 1 + 127 - (7 if fmt == "e4m3" else 14)
    else:
        mant, ex = np.frexp(amax / 6.0)
        byte = np.where(mant > 0.5, ex, ex - 1) + 127
    byte = np.clip(np.where(amax > 0, byte, 1), 1, 254)
    scaled = (w * np.exp2(127.0 - byte)[:, None, :]).reshape(k, n).astype(np.float32)
    by_word = np.ascontiguousarray(scaled.reshape(k // 512, 128, 4, n).transpose(0, 1, 3, 2))
    if fmt in ("e4m3", "e5m2"):
        words = by_word.astype(ml_dtypes.float8_e4m3fn if fmt == "e4m3" else ml_dtypes.float8_e5m2).view(np.uint8)
    else:
        c = by_word.astype(ml_dtypes.float4_e2m1fn).view(np.uint8) & 0xF
        words = (c[..., 0::2] | (c[..., 1::2] << 4)).reshape(k // 512, 128, 2 * n)
    return np.ascontiguousarray(words), np.ascontiguousarray(byte.astype(np.uint8).reshape(k // 512, 16, n))


def unpack_weight(words, scales, fmt):
    g, _, n = scales.shape
    words = np.ascontiguousarray(words).reshape(g, 128, n, -1)
    if fmt in ("e4m3", "e5m2"):
        vals = words.view(ml_dtypes.float8_e4m3fn if fmt == "e4m3" else ml_dtypes.float8_e5m2).astype(np.float64)
    else:
        nib = np.empty((g, 128, n, 4), np.uint8)
        nib[..., 0::2] = words & 0xF
        nib[..., 1::2] = words >> 4
        vals = E2M1[nib]
    vals = vals * np.repeat(np.exp2(scales.astype(np.float64) - 127.0), 8, axis=1)[..., None]
    return vals.transpose(0, 1, 3, 2).reshape(g * 512, n)


K, T, J, R, C, D, O, N, S = 512, 2048, 256, 512, 512, 512, 256, 256, 1024


def setup_inputs():
    n = np.random.standard_normal
    idx = np.random.permutation(T)[:J]
    idx2 = np.random.permutation(T)[:J]
    idx3 = np.random.permutation(C)[:J]
    idx4 = np.random.permutation(D)[:J]
    idx5 = np.random.permutation(D)[:C]
    idx6 = np.random.permutation(C)[:O]
    idx7 = np.random.permutation(S)[:N]
    fk = mx_kscale(K)
    fr = mx_kscale(R)
    xtp = pack_weight(n((K, T)) / fk[:, None], "e4m3")
    wp = pack_weight(n((K, R)) * 1 / np.sqrt(K) * fk[:, None] * fr, "e2m1")
    vsp = pack_weight(n((R, S)) * 1 / np.sqrt(R) / fr[:, None], "e5m2")
    return {
        "xt_words": xtp[0],
        "xt_scales": xtp[1],
        "w_words": wp[0],
        "w_scales": wp[1],
        "vs_words": vsp[0],
        "vs_scales": vsp[1],
        "offs": striped(idx),
        "offs2": striped(idx2),
        "offs3": striped(idx3),
        "offs4": striped(idx4),
        "offs5": striped(idx5),
        "offs6": striped(idx6),
        "offs7": striped(idx7),
    }


def reference(xt_words, xt_scales, w_words, w_scales, vs_words, vs_scales, offs, offs2, offs3, offs4, offs5, offs6, offs7):
    idx = unstriped(offs)
    idx2 = unstriped(offs2)
    idx3 = unstriped(offs3)
    idx4 = unstriped(offs4)
    idx5 = unstriped(offs5)
    idx6 = unstriped(offs6)
    idx7 = unstriped(offs7)
    xtu = unpack_weight(xt_words, xt_scales, "e4m3")
    wu = unpack_weight(w_words, w_scales, "e2m1")
    vsu = unpack_weight(vs_words, vs_scales, "e5m2")
    xtidxg = xtu[:, idx]
    a = wu.T @ xtidxg
    xtidx2g = xtu[:, idx2]
    b = wu.T @ xtidx2g
    pw = np.zeros((R, C))
    pw[:, idx3] = a
    pv = np.zeros((R, D))
    pv[:, idx4] = b
    pg = np.maximum(pw, pv[:, idx5])
    hid = pg[:, idx6]
    vsidx7g = vsu[:, idx7]
    hidq = mxq(hid, 0, "e4m3")
    y = vsidx7g.T @ hidq
    return y

@@ -1,0 +1,152 @@
+from contextlib import ExitStack
+
+import concourse.mybir as mybir
+
+K, T, J, R, C, O, N, S = 512, 2048, 256, 512, 512, 256, 256, 1024
+FLOPS = 2 * K * R * 2 * J + 2 * R * N * O
+
+F32 = mybir.dt.float32
+BF16 = mybir.dt.bfloat16
+I32 = mybir.dt.int32
+U32 = mybir.dt.uint32
+U16 = mybir.dt.uint16
+U8 = mybir.dt.uint8
+E4M3 = mybir.dt.float8_e4m3fn_x4
+E5M2 = mybir.dt.float8_e5m2_x4
+E2M1 = mybir.dt.float4_e2m1fn_x4
+COPY = mybir.ActivationFunctionType.Copy
+MAX = mybir.AluOpType.max
+P = 128
+
+
+def tile_list_boardsmeet_tied_store_plain_kernel(
+    tc, xt_words, xt_scales, w_words, w_scales, vs_words, vs_scales,
+    offs, offs2, offs3, offs4, offs5, offs6, offs7, out,
+):
+    nc = tc.nc
+    with ExitStack() as ctx:
+        lists = ctx.enter_context(tc.tile_pool(name="lists", bufs=1))
+        keep = ctx.enter_context(tc.tile_pool(name="keep", bufs=1))
+        psum = ctx.enter_context(tc.psum_pool(name="psum", bufs=8))
+
+        def move(on_scalar, dst, src):
+            if on_scalar:
+                nc.scalar.activation(dst, src, COPY)
+            else:
+                nc.vector.tensor_copy(dst, src)
+
+        def load_list(src, name):
+            t = lists.tile(list(src.shape), U16, name=name)
+            nc.sync.dma_start(t[:], src)
+            return t
+
+        def load_scales(queue, zero, src, name):
+            n = src.shape[2]
+            t = keep.tile([P, n], U8, name=name, align_bytes=64)
+            zero.memset(t[:].bitcast(I32), 0)
+            for q in range(4):
+                queue.dma_start(t[32 * q : 32 * q + 4, :].bitcast(I32), src[0, 4 * q : 4 * q + 4, :].bitcast(I32))
+            return t
+
+        l2 = load_list(offs2, "l2")
+        xs = load_scales(nc.scalar, nc.gpsimd, xt_scales, "xs")
+        ww = keep.tile([P, 2 * R], U8, name="ww", align_bytes=64)
+        nc.sync.dma_start(ww[:].bitcast(I32), w_words[0].bitcast(I32))
+        l1 = load_list(offs, "l1")
+        xw = keep.tile([P, T], I32, name="xw", align_bytes=64)
+        nc.sync.dma_start(xw[:], xt_words[0].rearrange("p n t -> p (n t)").bitcast(I32))
+        ws = load_scales(nc.sync, nc.gpsimd, w_scales, "ws")
+        l4 = load_list(offs4, "l4")
+        l3 = load_list(offs3, "l3")
+        l5 = load_list(offs5, "l5")
+
+        pv = [keep.tile([P, C], F32, name="pv%d" % t) for t in range(4)]
+        pw = [keep.tile([P, C], F32, name="pw%d" % t) for t in range(4)]
+        nc.vector.memset(pv[0][:], 0.0)
+        nc.vector.memset(pw[0][:], 0.0)
+        for t in range(1, 4):
+            nc.gpsimd.memset(pv[t][:], 0.0)
+            nc.gpsimd.memset(pw[t][:], 0.0)
+
+        vw = keep.tile([P, S], I32, name="vw", align_bytes=64)
+        nc.sync.dma_start(vw[:], vs_words[0].rearrange("p n t -> p (n t)").bitcast(I32))
+        l6 = load_list(offs6, "l6")
+        l7 = load_list(offs7, "l7")
+        vs = load_scales(nc.sync, nc.vector, vs_scales, "vs")
+
+        wd = keep.tile([P, 2 * R], U8, name="wd", align_bytes=64)
+        nc.vector.tensor_copy(
+            wd[:].bitcast(U16).rearrange("p (t m) -> p t m", t=4),
+            ww[:].bitcast(U16).rearrange("p (m t) -> p t m", t=4),
+        )
+        wsd = keep.tile([P, R], U8, name="wsd", align_bytes=64)
+        nc.vector.tensor_copy(
+            wsd[:].rearrange("p (t m) -> p t m", t=4), ws[:].rearrange("p (m t) -> p t m", t=4)
+        )
+
+        def pick(words, scales, lst, name):
+            gs = keep.tile([P, J], U8, name=name + "s", align_bytes=64)
+            nc.vector.tensor_copy(gs[:], scales[:].indirect(lst[:]))
+            gw = keep.tile([P, J], I32, name=name + "w", align_bytes=64)
+            nc.vector.tensor_copy(gw[:].bitcast(U32), words[:].bitcast(U32).indirect(lst[:]))
+            return gw, gs
+
+        def first_product(picked, t):
+            acc = psum.tile([P, 512], F32, name="acc")
+            nc.tensor.matmul_mx(
+                out=acc[:, :J],
+                lhsT=wd[:, 256 * t : 256 * (t + 1)].bitcast(E2M1),
+                lhsT_scale=wsd[:, 128 * t : 128 * (t + 1)],
+                rhs=picked[0][:].bitcast(E4M3),
+                rhs_scale=picked[1][:],
+                start=True,
+                stop=True,
+            )
+            return acc
+
+        xb = pick(xw, xs, l2, "xb")
+        xa = pick(xw, xs, l1, "xa")
+        b_acc = [first_product(xb, t) for t in range(4)]
+        a_acc = [first_product(xa, t) for t in range(4)]
+
+        def put(on_scalar, acc, board, lst, name):
+            vals = keep.tile([P, J], F32, name=name)
+            move(on_scalar, vals[:], acc[:, :J])
+            move(on_scalar, board[:].indirect(lst[:]), vals[:])
+
+        hg = keep.tile([P, 4, O], F32, name="hg", align_bytes=64)
+        pg = [keep.tile([P, C], F32, name="pg%d" % t) for t in range(4)]
+        vg = None
+        for t in range(4):
+            put(True, b_acc[t], pv[t], l4, "bv%d" % t)
+            put(t >= 2, a_acc[t], pw[t], l3, "av%d" % t)
+            g = keep.tile([P, C], F32, name="g%d" % t)
+            for h in range(2):
+                move(False, g[:, 256 * h : 256 * (h + 1)], pv[t][:].indirect(l5[:, 16 * h : 16 * (h + 1)]))
+            nc.vector.tensor_tensor(pg[t][:], pw[t][:], g[:], MAX)
+            if t == 1:
+                vg = pick(vw, vs, l7, "vg")
+        for t in range(4):
+            move(t in (1, 2), hg[:, t, :], pg[t][:].indirect(l6[:]))
+
+        hb = keep.tile([P, O, 4], BF16, name="hb", align_bytes=64)
+        for h in range(2):
+            cols = slice(128 * h, 128 * (h + 1))
+            move(h == 1, hb[:, cols, :], hg[:, :, cols].rearrange("p t o -> p o t"))
+        hq = keep.tile([P, O], U32, name="hq", align_bytes=64)
+        hs = keep.tile([P, O], U8, name="hs", align_bytes=64)
+        nc.vector.quantize_mx(out=hq[:].bitcast(E4M3), scales=hs[:], in_=hb[:].rearrange("p o t -> p (o t)"))
+        for u in range(2):
+            acc = psum.tile([P, 512], F32, name="acc")
+            nc.tensor.matmul_mx(
+                out=acc[:, :O],
+                lhsT=vg[0][:, 128 * u : 128 * (u + 1)].bitcast(E5M2),
+                lhsT_scale=vg[1][:, 128 * u : 128 * (u + 1)],
+                rhs=hq[:].bitcast(E4M3),
+                rhs_scale=hs[:],
+                start=True,
+                stop=True,
+            )
+            y = keep.tile([P, O], F32, name="y%d" % u)
+            move(u == 0, y[:], acc[:, :O])
+            (nc.scalar if u == 0 else nc.sync).dma_start(out[128 * u : 128 * (u + 1), :], y[:])

@@ -17,6 +17,8 @@ E2M1 = mybir.dt.float4_e2m1fn_x4
 COPY = mybir.ActivationFunctionType.Copy
 MAX = mybir.AluOpType.max
 P = 128
+WIDE = 704
+SPLIT = 160
 
 
 def tile_list_boardsmeet_tied_store_plain_kernel(
@@ -27,7 +29,7 @@ def tile_list_boardsmeet_tied_store_plain_kernel(
     with ExitStack() as ctx:
         lists = ctx.enter_context(tc.tile_pool(name="lists", bufs=1))
         keep = ctx.enter_context(tc.tile_pool(name="keep", bufs=1))
-        psum = ctx.enter_context(tc.psum_pool(name="psum", bufs=8))
+        psum = ctx.enter_context(tc.psum_pool(name="psum", bufs=1))
 
         def move(on_scalar, dst, src):
             if on_scalar:
@@ -49,104 +51,143 @@ def tile_list_boardsmeet_tied_store_plain_kernel(
             return t
 
         l2 = load_list(offs2, "l2")
-        xs = load_scales(nc.scalar, nc.gpsimd, xt_scales, "xs")
         ww = keep.tile([P, 2 * R], U8, name="ww", align_bytes=64)
         nc.sync.dma_start(ww[:].bitcast(I32), w_words[0].bitcast(I32))
         l1 = load_list(offs, "l1")
+        xs = load_scales(nc.sync, nc.gpsimd, xt_scales, "xs")
         xw = keep.tile([P, T], I32, name="xw", align_bytes=64)
         nc.sync.dma_start(xw[:], xt_words[0].rearrange("p n t -> p (n t)").bitcast(I32))
         ws = load_scales(nc.sync, nc.gpsimd, w_scales, "ws")
         l4 = load_list(offs4, "l4")
         l3 = load_list(offs3, "l3")
-        l5 = load_list(offs5, "l5")
-
-        pv = [keep.tile([P, C], F32, name="pv%d" % t) for t in range(4)]
-        pw = [keep.tile([P, C], F32, name="pw%d" % t) for t in range(4)]
-        nc.vector.memset(pv[0][:], 0.0)
-        nc.vector.memset(pw[0][:], 0.0)
-        for t in range(1, 4):
-            nc.gpsimd.memset(pv[t][:], 0.0)
-            nc.gpsimd.memset(pw[t][:], 0.0)
-
         vw = keep.tile([P, S], I32, name="vw", align_bytes=64)
         nc.sync.dma_start(vw[:], vs_words[0].rearrange("p n t -> p (n t)").bitcast(I32))
-        l6 = load_list(offs6, "l6")
+        l5 = load_list(offs5, "l5")
         l7 = load_list(offs7, "l7")
         vs = load_scales(nc.sync, nc.vector, vs_scales, "vs")
+        l6 = load_list(offs6, "l6")
+
+        pv = [keep.tile([P, WIDE], F32, name="pv%d" % t) for t in range(4)]
+        pw = [keep.tile([P, C], F32, name="pw%d" % t) for t in range(4)]
+        for t in range(4):
+            zero = nc.vector if t < 2 else nc.gpsimd
+            zero.memset(pv[t][:], 0.0)
+            zero.memset(pw[t][:], 0.0)
 
         wd = keep.tile([P, 2 * R], U8, name="wd", align_bytes=64)
         nc.vector.tensor_copy(
             wd[:].bitcast(U16).rearrange("p (t m) -> p t m", t=4),
             ww[:].bitcast(U16).rearrange("p (m t) -> p t m", t=4),
         )
+        gs = keep.tile([P, 2 * J], U8, name="gs", align_bytes=64)
+        gw = keep.tile([P, 2 * J], I32, name="gw", align_bytes=64)
+        nc.vector.tensor_copy(gs[:, :J], xs[:].indirect(l2[:]))
+        nc.vector.tensor_copy(gs[:, J:], xs[:].indirect(l1[:]))
+        nc.vector.tensor_copy(gw[:, :J].bitcast(U32), xw[:].bitcast(U32).indirect(l2[:]))
         wsd = keep.tile([P, R], U8, name="wsd", align_bytes=64)
-        nc.vector.tensor_copy(
-            wsd[:].rearrange("p (t m) -> p t m", t=4), ws[:].rearrange("p (m t) -> p t m", t=4)
-        )
+        for part in (slice(0, 1), slice(1, 4)):
+            nc.gpsimd.tensor_copy(
+                wsd[:].rearrange("p (t m) -> p t m", t=4)[:, part, :], ws[:].rearrange("p (m t) -> p t m", t=4)[:, part, :]
+            )
+        nc.vector.tensor_copy(gw[:, J:].bitcast(U32), xw[:].bitcast(U32).indirect(l1[:]))
 
-        def pick(words, scales, lst, name):
-            gs = keep.tile([P, J], U8, name=name + "s", align_bytes=64)
-            nc.vector.tensor_copy(gs[:], scales[:].indirect(lst[:]))
-            gw = keep.tile([P, J], I32, name=name + "w", align_bytes=64)
-            nc.vector.tensor_copy(gw[:].bitcast(U32), words[:].bitcast(U32).indirect(lst[:]))
-            return gw, gs
-
-        def first_product(picked, t):
-            acc = psum.tile([P, 512], F32, name="acc")
+        def first_product(acc, t, cols):
             nc.tensor.matmul_mx(
-                out=acc[:, :J],
+                out=acc,
                 lhsT=wd[:, 256 * t : 256 * (t + 1)].bitcast(E2M1),
                 lhsT_scale=wsd[:, 128 * t : 128 * (t + 1)],
-                rhs=picked[0][:].bitcast(E4M3),
-                rhs_scale=picked[1][:],
+                rhs=gw[:, cols].bitcast(E4M3),
+                rhs_scale=gs[:, cols],
                 start=True,
                 stop=True,
             )
-            return acc
 
-        xb = pick(xw, xs, l2, "xb")
-        xa = pick(xw, xs, l1, "xa")
-        b_acc = [first_product(xb, t) for t in range(4)]
-        a_acc = [first_product(xa, t) for t in range(4)]
+        B, A = slice(0, J), slice(J, 2 * J)
+        acc_b0 = psum.tile([P, J], F32, name="acc_b0")
+        acc_b1 = psum.tile([P, J], F32, name="acc_b1")
+        acc_a01 = psum.tile([P, 2 * J], F32, name="acc_a01")
+        acc_2 = psum.tile([P, 2 * J], F32, name="acc_2")
+        acc_3 = psum.tile([P, 2 * J], F32, name="acc_3")
+        first_product(acc_b0[:], 0, B)
+        first_product(acc_b1[:], 1, B)
+        first_product(acc_a01[:, :J], 0, A)
+        first_product(acc_a01[:, J:], 1, A)
+        first_product(acc_2[:], 2, slice(0, 2 * J))
+        first_product(acc_3[:], 3, slice(0, 2 * J))
 
-        def put(on_scalar, acc, board, lst, name):
-            vals = keep.tile([P, J], F32, name=name)
-            move(on_scalar, vals[:], acc[:, :J])
-            move(on_scalar, board[:].indirect(lst[:]), vals[:])
+        b0 = keep.tile([P, J], F32, name="b0")
+        b1 = keep.tile([P, J], F32, name="b1")
+        a01 = keep.tile([P, 2 * J], F32, name="a01")
+        ba2 = keep.tile([P, 2 * J], F32, name="ba2")
+        ba3 = keep.tile([P, 2 * J], F32, name="ba3")
+        b_vals = [b0[:], b1[:], ba2[:, B], ba3[:, B]]
+        a_vals = [a01[:, :J], a01[:, J:], ba2[:, A], ba3[:, A]]
 
         hg = keep.tile([P, 4, O], F32, name="hg", align_bytes=64)
         pg = [keep.tile([P, C], F32, name="pg%d" % t) for t in range(4)]
-        vg = None
+        g = [keep.tile([P, C], F32, name="g%d" % t) for t in range(4)]
+        vgs = keep.tile([P, N], U8, name="vgs", align_bytes=64)
+        vgw = keep.tile([P, N], I32, name="vgw", align_bytes=64)
+
+        def put_b(t):
+            move(t != 1, pv[t][:].indirect(l4[:]), b_vals[t])
+
+        def put_a(t):
+            move(t != 1, pw[t][:].indirect(l3[:]), a_vals[t])
+
+        def look(t):
+            move(False, g[t][:], pv[t][:].indirect(l5[:]))
+
+        def larger(t):
+            nc.vector.tensor_tensor(pg[t][:], pw[t][:], g[t][:], MAX)
+
+        def read(t):
+            move(t < 2, hg[:, t, :], pg[t][:].indirect(l6[:]))
+
+        move(True, b0[:], acc_b0[:])
+        move(False, b1[:], acc_b1[:])
+        put_b(0)
+        put_b(1)
+        move(True, a01[:], acc_a01[:])
+        move(True, ba2[:], acc_2[:])
+        look(0)
+        put_a(0)
+        move(False, ba3[:], acc_3[:])
+        look(1)
+        put_b(2)
+        put_a(1)
+        larger(0)
+        put_a(2)
+        nc.vector.tensor_copy(vgw[:].bitcast(U32), vw[:].bitcast(U32).indirect(l7[:]))
+        larger(1)
+        put_b(3)
+        look(2)
+        nc.vector.tensor_copy(vgs[:], vs[:].indirect(l7[:]))
+        larger(2)
+        put_a(3)
+        look(3)
+        larger(3)
         for t in range(4):
-            put(True, b_acc[t], pv[t], l4, "bv%d" % t)
-            put(t >= 2, a_acc[t], pw[t], l3, "av%d" % t)
-            g = keep.tile([P, C], F32, name="g%d" % t)
-            for h in range(2):
-                move(False, g[:, 256 * h : 256 * (h + 1)], pv[t][:].indirect(l5[:, 16 * h : 16 * (h + 1)]))
-            nc.vector.tensor_tensor(pg[t][:], pw[t][:], g[:], MAX)
-            if t == 1:
-                vg = pick(vw, vs, l7, "vg")
-        for t in range(4):
-            move(t in (1, 2), hg[:, t, :], pg[t][:].indirect(l6[:]))
+            read(t)
 
         hb = keep.tile([P, O, 4], BF16, name="hb", align_bytes=64)
         for h in range(2):
-            cols = slice(128 * h, 128 * (h + 1))
+            cols = slice(0, SPLIT) if h == 0 else slice(SPLIT, O)
             move(h == 1, hb[:, cols, :], hg[:, :, cols].rearrange("p t o -> p o t"))
         hq = keep.tile([P, O], U32, name="hq", align_bytes=64)
         hs = keep.tile([P, O], U8, name="hs", align_bytes=64)
         nc.vector.quantize_mx(out=hq[:].bitcast(E4M3), scales=hs[:], in_=hb[:].rearrange("p o t -> p (o t)"))
         for u in range(2):
-            acc = psum.tile([P, 512], F32, name="acc")
+            yacc = psum.tile([P, O], F32, name="yacc%d" % u)
             nc.tensor.matmul_mx(
-                out=acc[:, :O],
-                lhsT=vg[0][:, 128 * u : 128 * (u + 1)].bitcast(E5M2),
-                lhsT_scale=vg[1][:, 128 * u : 128 * (u + 1)],
+                out=yacc[:],
+                lhsT=vgw[:, 128 * u : 128 * (u + 1)].bitcast(E5M2),
+                lhsT_scale=vgs[:, 128 * u : 128 * (u + 1)],
                 rhs=hq[:].bitcast(E4M3),
                 rhs_scale=hs[:],
                 start=True,
                 stop=True,
             )
             y = keep.tile([P, O], F32, name="y%d" % u)
-            move(u == 0, y[:], acc[:, :O])
+            move(u == 0, y[:], yacc[:])
             (nc.scalar if u == 0 else nc.sync).dma_start(out[128 * u : 128 * (u + 1), :], y[:])

@@ -17,8 +17,6 @@ E2M1 = mybir.dt.float4_e2m1fn_x4
 COPY = mybir.ActivationFunctionType.Copy
 MAX = mybir.AluOpType.max
 P = 128
-WIDE = 704
-SPLIT = 160
 
 
 def tile_list_boardsmeet_tied_store_plain_kernel(
@@ -42,9 +40,9 @@ def tile_list_boardsmeet_tied_store_plain_kernel(
             nc.sync.dma_start(t[:], src)
             return t
 
-        def load_scales(queue, zero, src, name):
+        def load_scales(queue, zero, src, name, tag=None):
             n = src.shape[2]
-            t = keep.tile([P, n], U8, name=name, align_bytes=64)
+            t = keep.tile([P, n], U8, name=name, tag=tag or name, align_bytes=64)
             zero.memset(t[:].bitcast(I32), 0)
             for q in range(4):
                 queue.dma_start(t[32 * q : 32 * q + 4, :].bitcast(I32), src[0, 4 * q : 4 * q + 4, :].bitcast(I32))
@@ -57,22 +55,23 @@ def tile_list_boardsmeet_tied_store_plain_kernel(
         xs = load_scales(nc.sync, nc.gpsimd, xt_scales, "xs")
         xw = keep.tile([P, T], I32, name="xw", align_bytes=64)
         nc.sync.dma_start(xw[:], xt_words[0].rearrange("p n t -> p (n t)").bitcast(I32))
-        ws = load_scales(nc.sync, nc.gpsimd, w_scales, "ws")
+        ws = load_scales(nc.sync, nc.gpsimd, w_scales, "ws", "shared")
         l4 = load_list(offs4, "l4")
-        l3 = load_list(offs3, "l3")
+        l7 = load_list(offs7, "l7")
         vw = keep.tile([P, S], I32, name="vw", align_bytes=64)
         nc.sync.dma_start(vw[:], vs_words[0].rearrange("p n t -> p (n t)").bitcast(I32))
         l5 = load_list(offs5, "l5")
-        l7 = load_list(offs7, "l7")
-        vs = load_scales(nc.sync, nc.vector, vs_scales, "vs")
+        l3 = load_list(offs3, "l3")
+        vs = load_scales(nc.sync, nc.gpsimd, vs_scales, "vs")
         l6 = load_list(offs6, "l6")
 
-        pv = [keep.tile([P, WIDE], F32, name="pv%d" % t) for t in range(4)]
-        pw = [keep.tile([P, C], F32, name="pw%d" % t) for t in range(4)]
-        for t in range(4):
-            zero = nc.vector if t < 2 else nc.gpsimd
-            zero.memset(pv[t][:], 0.0)
-            zero.memset(pw[t][:], 0.0)
+        def board(on_vector, name):
+            t = keep.tile([P, C + 1 if on_vector else C], F32, name=name)
+            (nc.vector if on_vector else nc.gpsimd).memset(t[:], 0.0)
+            return t
+
+        pv = [board(t < 3, "pv%d" % t) for t in range(4)]
+        pw = [board(t < 2, "pw%d" % t) for t in range(4)]
 
         wd = keep.tile([P, 2 * R], U8, name="wd", align_bytes=64)
         nc.vector.tensor_copy(
@@ -80,23 +79,24 @@ def tile_list_boardsmeet_tied_store_plain_kernel(
             ww[:].bitcast(U16).rearrange("p (m t) -> p t m", t=4),
         )
         gs = keep.tile([P, 2 * J], U8, name="gs", align_bytes=64)
-        gw = keep.tile([P, 2 * J], I32, name="gw", align_bytes=64)
         nc.vector.tensor_copy(gs[:, :J], xs[:].indirect(l2[:]))
         nc.vector.tensor_copy(gs[:, J:], xs[:].indirect(l1[:]))
-        nc.vector.tensor_copy(gw[:, :J].bitcast(U32), xw[:].bitcast(U32).indirect(l2[:]))
+        gwb = keep.tile([P, J], I32, name="gwb", align_bytes=64)
+        nc.vector.tensor_copy(gwb[:].bitcast(U32), xw[:].bitcast(U32).indirect(l2[:]))
         wsd = keep.tile([P, R], U8, name="wsd", align_bytes=64)
-        for part in (slice(0, 1), slice(1, 4)):
-            nc.gpsimd.tensor_copy(
+        for part in (slice(0, 2), slice(2, 4)):
+            nc.vector.tensor_copy(
                 wsd[:].rearrange("p (t m) -> p t m", t=4)[:, part, :], ws[:].rearrange("p (m t) -> p t m", t=4)[:, part, :]
             )
-        nc.vector.tensor_copy(gw[:, J:].bitcast(U32), xw[:].bitcast(U32).indirect(l1[:]))
+        gwa = keep.tile([P, J], I32, name="gwa", tag="shared", align_bytes=64)
+        nc.vector.tensor_copy(gwa[:].bitcast(U32), xw[:].bitcast(U32).indirect(l1[:]))
 
         def first_product(acc, t, cols):
             nc.tensor.matmul_mx(
                 out=acc,
                 lhsT=wd[:, 256 * t : 256 * (t + 1)].bitcast(E2M1),
                 lhsT_scale=wsd[:, 128 * t : 128 * (t + 1)],
-                rhs=gw[:, cols].bitcast(E4M3),
+                rhs=(gwb if cols.start == 0 else gwa)[:].bitcast(E4M3),
                 rhs_scale=gs[:, cols],
                 start=True,
                 stop=True,
@@ -112,18 +112,19 @@ def tile_list_boardsmeet_tied_store_plain_kernel(
         first_product(acc_b1[:], 1, B)
         first_product(acc_a01[:, :J], 0, A)
         first_product(acc_a01[:, J:], 1, A)
-        first_product(acc_2[:], 2, slice(0, 2 * J))
-        first_product(acc_3[:], 3, slice(0, 2 * J))
+        for t, acc in ((2, acc_2), (3, acc_3)):
+            first_product(acc[:, B], t, B)
+            first_product(acc[:, A], t, A)
 
         b0 = keep.tile([P, J], F32, name="b0")
-        b1 = keep.tile([P, J], F32, name="b1")
+        b1 = keep.tile([P, J], F32, name="b1", tag="vals")
         a01 = keep.tile([P, 2 * J], F32, name="a01")
         ba2 = keep.tile([P, 2 * J], F32, name="ba2")
-        ba3 = keep.tile([P, 2 * J], F32, name="ba3")
-        b_vals = [b0[:], b1[:], ba2[:, B], ba3[:, B]]
-        a_vals = [a01[:, :J], a01[:, J:], ba2[:, A], ba3[:, A]]
+        b_vals = [b0[:], b1[:], ba2[:, B]]
+        a_vals = [a01[:, :J], a01[:, J:], ba2[:, A]]
 
-        hg = keep.tile([P, 4, O], F32, name="hg", align_bytes=64)
+        hg = [keep.tile([P, 2, 128], BF16, name="hg%d" % h, align_bytes=64) for h in range(2)]
+        hb = [keep.tile([P, 128, 4], BF16, name="hb%d" % h, align_bytes=64) for h in range(2)]
         pg = [keep.tile([P, C], F32, name="pg%d" % t) for t in range(4)]
         g = [keep.tile([P, C], F32, name="g%d" % t) for t in range(4)]
         vgs = keep.tile([P, N], U8, name="vgs", align_bytes=64)
@@ -136,58 +137,69 @@ def tile_list_boardsmeet_tied_store_plain_kernel(
             move(t != 1, pw[t][:].indirect(l3[:]), a_vals[t])
 
         def look(t):
-            move(False, g[t][:], pv[t][:].indirect(l5[:]))
+            for h in range(2):
+                move(t == 3 and h == 1, g[t][:, 256 * h : 256 * (h + 1)], pv[t][:].indirect(l5[:, 16 * h : 16 * (h + 1)]))
 
         def larger(t):
-            nc.vector.tensor_tensor(pg[t][:], pw[t][:], g[t][:], MAX)
+            nc.vector.tensor_tensor(pg[t][:], pw[t][:, :C], g[t][:], MAX)
 
-        def read(t):
-            move(t < 2, hg[:, t, :], pg[t][:].indirect(l6[:]))
+        def read(on_scalar, t, h):
+            dst = hg[h][:, t, :] if t < 2 else hb[h][:, :, t]
+            move(on_scalar, dst, pg[t][:].indirect(l6[:, 8 * h : 8 * (h + 1)]))
 
         move(True, b0[:], acc_b0[:])
-        move(False, b1[:], acc_b1[:])
+        move(True, b1[:], acc_b1[:])
+        nc.vector.tensor_copy(vgw[:].bitcast(U32), vw[:].bitcast(U32).indirect(l7[:]))
         put_b(0)
         put_b(1)
         move(True, a01[:], acc_a01[:])
         move(True, ba2[:], acc_2[:])
         look(0)
         put_a(0)
-        move(False, ba3[:], acc_3[:])
         look(1)
         put_b(2)
         put_a(1)
+        ba3 = keep.tile([P, 2 * J], F32, name="ba3", tag="vals")
+        b_vals.append(ba3[:, B])
+        a_vals.append(ba3[:, A])
+        move(False, ba3[:], acc_3[:])
         larger(0)
         put_a(2)
-        nc.vector.tensor_copy(vgw[:].bitcast(U32), vw[:].bitcast(U32).indirect(l7[:]))
         larger(1)
         put_b(3)
         look(2)
         nc.vector.tensor_copy(vgs[:], vs[:].indirect(l7[:]))
         larger(2)
         put_a(3)
+        read(False, 2, 0)
+        read(False, 2, 1)
         look(3)
         larger(3)
-        for t in range(4):
-            read(t)
+        read(True, 0, 0)
+        read(True, 1, 0)
+        read(True, 0, 1)
+        nc.scalar.copy(hb[0][:, :, 0:2], hg[0][:].rearrange("p t o -> p o t"))
+        read(True, 1, 1)
+        nc.scalar.copy(hb[1][:, :, 0:2], hg[1][:].rearrange("p t o -> p o t"))
+        read(False, 3, 0)
+        read(False, 3, 1)
 
-        hb = keep.tile([P, O, 4], BF16, name="hb", align_bytes=64)
+        out_rows = out.rearrange("(u p) o -> p u o", p=P)
         for h in range(2):
-            cols = slice(0, SPLIT) if h == 0 else slice(SPLIT, O)
-            move(h == 1, hb[:, cols, :], hg[:, :, cols].rearrange("p t o -> p o t"))
-        hq = keep.tile([P, O], U32, name="hq", align_bytes=64)
-        hs = keep.tile([P, O], U8, name="hs", align_bytes=64)
-        nc.vector.quantize_mx(out=hq[:].bitcast(E4M3), scales=hs[:], in_=hb[:].rearrange("p o t -> p (o t)"))
-        for u in range(2):
-            yacc = psum.tile([P, O], F32, name="yacc%d" % u)
-            nc.tensor.matmul_mx(
-                out=yacc[:],
-                lhsT=vgw[:, 128 * u : 128 * (u + 1)].bitcast(E5M2),
-                lhsT_scale=vgs[:, 128 * u : 128 * (u + 1)],
-                rhs=hq[:].bitcast(E4M3),
-                rhs_scale=hs[:],
-                start=True,
-                stop=True,
-            )
-            y = keep.tile([P, O], F32, name="y%d" % u)
-            move(u == 0, y[:], yacc[:])
-            (nc.scalar if u == 0 else nc.sync).dma_start(out[128 * u : 128 * (u + 1), :], y[:])
+            hq = keep.tile([P, 128], U32, name="hq%d" % h, align_bytes=64)
+            hs = keep.tile([P, 128], U8, name="hs%d" % h, align_bytes=64)
+            nc.vector.quantize_mx(out=hq[:].bitcast(E4M3), scales=hs[:], in_=hb[h][:].rearrange("p o t -> p (o t)"))
+            yacc = psum.tile([P, 2, 128], F32, name="yacc%d" % h)
+            for u in range(2):
+                nc.tensor.matmul_mx(
+                    out=yacc[:, u, :],
+                    lhsT=vgw[:, 128 * u : 128 * (u + 1)].bitcast(E5M2),
+                    lhsT_scale=vgs[:, 128 * u : 128 * (u + 1)],
+                    rhs=hq[:].bitcast(E4M3),
+                    rhs_scale=hs[:],
+                    start=True,
+                    stop=True,
+                )
+            y = keep.tile([P, 2, 128], F32, name="y%d" % h)
+            move(h == 0, y[:], yacc[:])
+            (nc.scalar if h == 0 else nc.sync).dma_start(out_rows[:, :, 128 * h : 128 * (h + 1)], y[:])

from contextlib import ExitStack

import concourse.mybir as mybir

K, T, J, R, C, O, N, S = 512, 2048, 256, 512, 512, 256, 256, 1024
FLOPS = 2 * K * R * 2 * J + 2 * R * N * O

F32 = mybir.dt.float32
BF16 = mybir.dt.bfloat16
I32 = mybir.dt.int32
U32 = mybir.dt.uint32
U16 = mybir.dt.uint16
U8 = mybir.dt.uint8
E4M3 = mybir.dt.float8_e4m3fn_x4
E5M2 = mybir.dt.float8_e5m2_x4
E2M1 = mybir.dt.float4_e2m1fn_x4
COPY = mybir.ActivationFunctionType.Copy
MAX = mybir.AluOpType.max
P = 128


def tile_list_boardsmeet_tied_store_plain_kernel(
    tc, xt_words, xt_scales, w_words, w_scales, vs_words, vs_scales,
    offs, offs2, offs3, offs4, offs5, offs6, offs7, out,
):
    nc = tc.nc
    with ExitStack() as ctx:
        lists = ctx.enter_context(tc.tile_pool(name="lists", bufs=1))
        keep = ctx.enter_context(tc.tile_pool(name="keep", bufs=1))
        psum = ctx.enter_context(tc.psum_pool(name="psum", bufs=1))

        def move(on_scalar, dst, src):
            if on_scalar:
                nc.scalar.activation(dst, src, COPY)
            else:
                nc.vector.tensor_copy(dst, src)

        def load_list(src, name):
            t = lists.tile(list(src.shape), U16, name=name)
            nc.sync.dma_start(t[:], src)
            return t

        def load_scales(queue, zero, src, name, tag=None):
            n = src.shape[2]
            t = keep.tile([P, n], U8, name=name, tag=tag or name, align_bytes=64)
            zero.memset(t[:].bitcast(I32), 0)
            for q in range(4):
                queue.dma_start(t[32 * q : 32 * q + 4, :].bitcast(I32), src[0, 4 * q : 4 * q + 4, :].bitcast(I32))
            return t

        l2 = load_list(offs2, "l2")
        ww = keep.tile([P, 2 * R], U8, name="ww", align_bytes=64)
        nc.sync.dma_start(ww[:].bitcast(I32), w_words[0].bitcast(I32))
        l1 = load_list(offs, "l1")
        xs = load_scales(nc.sync, nc.gpsimd, xt_scales, "xs")
        xw = keep.tile([P, T], I32, name="xw", align_bytes=64)
        nc.sync.dma_start(xw[:], xt_words[0].rearrange("p n t -> p (n t)").bitcast(I32))
        ws = load_scales(nc.sync, nc.gpsimd, w_scales, "ws", "shared")
        l4 = load_list(offs4, "l4")
        l7 = load_list(offs7, "l7")
        vw = keep.tile([P, S], I32, name="vw", align_bytes=64)
        nc.sync.dma_start(vw[:], vs_words[0].rearrange("p n t -> p (n t)").bitcast(I32))
        l5 = load_list(offs5, "l5")
        l3 = load_list(offs3, "l3")
        vs = load_scales(nc.sync, nc.gpsimd, vs_scales, "vs")
        l6 = load_list(offs6, "l6")

        def board(on_vector, name):
            t = keep.tile([P, C + 1 if on_vector else C], F32, name=name)
            (nc.vector if on_vector else nc.gpsimd).memset(t[:], 0.0)
            return t

        pv = [board(t < 3, "pv%d" % t) for t in range(4)]
        pw = [board(t < 2, "pw%d" % t) for t in range(4)]

        wd = keep.tile([P, 2 * R], U8, name="wd", align_bytes=64)
        nc.vector.tensor_copy(
            wd[:].bitcast(U16).rearrange("p (t m) -> p t m", t=4),
            ww[:].bitcast(U16).rearrange("p (m t) -> p t m", t=4),
        )
        gs = keep.tile([P, 2 * J], U8, name="gs", align_bytes=64)
        nc.vector.tensor_copy(gs[:, :J], xs[:].indirect(l2[:]))
        nc.vector.tensor_copy(gs[:, J:], xs[:].indirect(l1[:]))
        gwb = keep.tile([P, J], I32, name="gwb", align_bytes=64)
        nc.vector.tensor_copy(gwb[:].bitcast(U32), xw[:].bitcast(U32).indirect(l2[:]))
        wsd = keep.tile([P, R], U8, name="wsd", align_bytes=64)
        for part in (slice(0, 2), slice(2, 4)):
            nc.vector.tensor_copy(
                wsd[:].rearrange("p (t m) -> p t m", t=4)[:, part, :], ws[:].rearrange("p (m t) -> p t m", t=4)[:, part, :]
            )
        gwa = keep.tile([P, J], I32, name="gwa", tag="shared", align_bytes=64)
        nc.vector.tensor_copy(gwa[:].bitcast(U32), xw[:].bitcast(U32).indirect(l1[:]))

        def first_product(acc, t, cols):
            nc.tensor.matmul_mx(
                out=acc,
                lhsT=wd[:, 256 * t : 256 * (t + 1)].bitcast(E2M1),
                lhsT_scale=wsd[:, 128 * t : 128 * (t + 1)],
                rhs=(gwb if cols.start == 0 else gwa)[:].bitcast(E4M3),
                rhs_scale=gs[:, cols],
                start=True,
                stop=True,
            )

        B, A = slice(0, J), slice(J, 2 * J)
        acc_b0 = psum.tile([P, J], F32, name="acc_b0")
        acc_b1 = psum.tile([P, J], F32, name="acc_b1")
        acc_a01 = psum.tile([P, 2 * J], F32, name="acc_a01")
        acc_2 = psum.tile([P, 2 * J], F32, name="acc_2")
        acc_3 = psum.tile([P, 2 * J], F32, name="acc_3")
        first_product(acc_b0[:], 0, B)
        first_product(acc_b1[:], 1, B)
        first_product(acc_a01[:, :J], 0, A)
        first_product(acc_a01[:, J:], 1, A)
        for t, acc in ((2, acc_2), (3, acc_3)):
            first_product(acc[:, B], t, B)
            first_product(acc[:, A], t, A)

        b0 = keep.tile([P, J], F32, name="b0")
        b1 = keep.tile([P, J], F32, name="b1", tag="vals")
        a01 = keep.tile([P, 2 * J], F32, name="a01")
        ba2 = keep.tile([P, 2 * J], F32, name="ba2")
        b_vals = [b0[:], b1[:], ba2[:, B]]
        a_vals = [a01[:, :J], a01[:, J:], ba2[:, A]]

        hg = [keep.tile([P, 2, 128], BF16, name="hg%d" % h, align_bytes=64) for h in range(2)]
        hb = [keep.tile([P, 128, 4], BF16, name="hb%d" % h, align_bytes=64) for h in range(2)]
        pg = [keep.tile([P, C], F32, name="pg%d" % t) for t in range(4)]
        g = [keep.tile([P, C], F32, name="g%d" % t) for t in range(4)]
        vgs = keep.tile([P, N], U8, name="vgs", align_bytes=64)
        vgw = keep.tile([P, N], I32, name="vgw", align_bytes=64)

        def put_b(t):
            move(t != 1, pv[t][:].indirect(l4[:]), b_vals[t])

        def put_a(t):
            move(t != 1, pw[t][:].indirect(l3[:]), a_vals[t])

        def look(t):
            for h in range(2):
                move(t == 3 and h == 1, g[t][:, 256 * h : 256 * (h + 1)], pv[t][:].indirect(l5[:, 16 * h : 16 * (h + 1)]))

        def larger(t):
            nc.vector.tensor_tensor(pg[t][:], pw[t][:, :C], g[t][:], MAX)

        def read(on_scalar, t, h):
            dst = hg[h][:, t, :] if t < 2 else hb[h][:, :, t]
            move(on_scalar, dst, pg[t][:].indirect(l6[:, 8 * h : 8 * (h + 1)]))

        move(True, b0[:], acc_b0[:])
        move(True, b1[:], acc_b1[:])
        nc.vector.tensor_copy(vgw[:].bitcast(U32), vw[:].bitcast(U32).indirect(l7[:]))
        put_b(0)
        put_b(1)
        move(True, a01[:], acc_a01[:])
        move(True, ba2[:], acc_2[:])
        look(0)
        put_a(0)
        look(1)
        put_b(2)
        put_a(1)
        ba3 = keep.tile([P, 2 * J], F32, name="ba3", tag="vals")
        b_vals.append(ba3[:, B])
        a_vals.append(ba3[:, A])
        move(False, ba3[:], acc_3[:])
        larger(0)
        put_a(2)
        larger(1)
        put_b(3)
        look(2)
        nc.vector.tensor_copy(vgs[:], vs[:].indirect(l7[:]))
        larger(2)
        put_a(3)
        read(False, 2, 0)
        read(False, 2, 1)
        look(3)
        larger(3)
        read(True, 0, 0)
        read(True, 1, 0)
        read(True, 0, 1)
        nc.scalar.copy(hb[0][:, :, 0:2], hg[0][:].rearrange("p t o -> p o t"))
        read(True, 1, 1)
        nc.scalar.copy(hb[1][:, :, 0:2], hg[1][:].rearrange("p t o -> p o t"))
        read(False, 3, 0)
        read(False, 3, 1)

        out_rows = out.rearrange("(u p) o -> p u o", p=P)
        for h in range(2):
            hq = keep.tile([P, 128], U32, name="hq%d" % h, align_bytes=64)
            hs = keep.tile([P, 128], U8, name="hs%d" % h, align_bytes=64)
            nc.vector.quantize_mx(out=hq[:].bitcast(E4M3), scales=hs[:], in_=hb[h][:].rearrange("p o t -> p (o t)"))
            yacc = psum.tile([P, 2, 128], F32, name="yacc%d" % h)
            for u in range(2):
                nc.tensor.matmul_mx(
                    out=yacc[:, u, :],
                    lhsT=vgw[:, 128 * u : 128 * (u + 1)].bitcast(E5M2),
                    lhsT_scale=vgs[:, 128 * u : 128 * (u + 1)],
                    rhs=hq[:].bitcast(E4M3),
                    rhs_scale=hs[:],
                    start=True,
                    stop=True,
                )
            y = keep.tile([P, 2, 128], F32, name="y%d" % h)
            move(h == 0, y[:], yacc[:])
            (nc.scalar if h == 0 else nc.sync).dma_start(out_rows[:, :, 128 * h : 128 * (h + 1)], y[:])
